import numpy as np
import ml_dtypes


def mxq(x, axis, fmt="e4m3"):
    dtype, down = {"e4m3": (ml_dtypes.float8_e4m3fn, 7), "e5m2": (ml_dtypes.float8_e5m2, 14)}[fmt]
    v = np.moveaxis(np.asarray(x, np.float32).astype(ml_dtypes.bfloat16).astype(np.float64), axis, -1)
    blocks = v.reshape(v.shape[:-1] + (-1, 32))
    amax = np.abs(blocks).max(-1, keepdims=True)
    byte = np.maximum(np.where(amax > 0, np.frexp(amax)[1] - 1 + 127, 0) - down, 1)
    scale = np.exp2(byte - 127.0)
    codes = (blocks / scale).astype(np.float32).astype(dtype).astype(np.float64)
    return np.moveaxis((codes * scale).reshape(v.shape), -1, axis)


WIDE = False


def mx_kscale(k):
    if not WIDE:
        return np.ones(k)
    levels = np.array([10, -10, 5, -5, 0])
    if k % 512:
        return np.exp2(np.random.permutation(np.resize(levels, k // 32))).repeat(32)
    a = np.empty((k // 512, 16))
    for p in range(k // 512):
        a[p, :8] = np.random.permutation(np.resize(levels, 8))
        for g in range(8):
            far = levels[np.abs(levels - a[p, g]) >= 10]
            a[p, g + 8] = far[np.random.randint(len(far))]
    return np.exp2(a.ravel()).repeat(32)


def f64(x):
    return np.asarray(x).astype(np.float64)


def striped(idx):
    return np.tile(idx.reshape(-1, 16).T, (8, 1)).astype(np.uint16)


def unstriped(offs):
    return offs[:16].T.reshape(-1).astype(np.int64)


E2M1 = np.array([0.0, 0.5, 1.0, 1.5, 2.0, 3.0, 4.0, 6.0, -0.0, -0.5, -1.0, -1.5, -2.0, -3.0, -4.0, -6.0])


def pack_weight(w, fmt):
    k, n = w.shape
    w = f64(np.asarray(w, np.float32).astype(ml_dtypes.bfloat16)).reshape(k // 32, 32, n)
    amax = np.abs(w).max(1)
    if fmt == "e4m3":
        byte = np.frexp(amax)[1] - 1 + 127 - 7
    else:
        mant, ex = np.frexp(amax / 6.0)
        byte = np.where(mant > 0.5, ex, ex - 1) + 127
    byte = np.clip(np.where(amax > 0, byte, 1), 1, 254)
    scaled = (w * np.exp2(127.0 - byte)[:, None, :]).reshape(k, n).astype(np.float32)
    by_word = np.ascontiguousarray(scaled.reshape(k // 512, 128, 4, n).transpose(0, 1, 3, 2))
    if fmt == "e4m3":
        words = by_word.astype(ml_dtypes.float8_e4m3fn).view(np.uint8)
    else:
        c = by_word.astype(ml_dtypes.float4_e2m1fn).view(np.uint8) & 0xF
        words = (c[..., 0::2] | (c[..., 1::2] << 4)).reshape(k // 512, 128, 2 * n)
    return np.ascontiguousarray(words), np.ascontiguousarray(byte.astype(np.uint8).reshape(k // 512, 16, n))


def unpack_weight(words, scales, fmt):
    g, _, n = scales.shape
    words = np.ascontiguousarray(words).reshape(g, 128, n, -1)
    if fmt == "e4m3":
        vals = words.view(ml_dtypes.float8_e4m3fn).astype(np.float64)
    else:
        nib = np.empty((g, 128, n, 4), np.uint8)
        nib[..., 0::2] = words & 0xF
        nib[..., 1::2] = words >> 4
        vals = E2M1[nib]
    vals = vals * np.repeat(np.exp2(scales.astype(np.float64) - 127.0), 8, axis=1)[..., None]
    return vals.transpose(0, 1, 3, 2).reshape(g * 512, n)


def gelu(v):
    return 0.5 * v * (1.0 + np.tanh(np.sqrt(2.0 / np.pi) * (v + 0.044715 * v**3)))


K, M, H, N, S, T, T2 = 1024, 512, 1024, 512, 512, 2048, 1024

def setup_inputs():
    n = np.random.standard_normal
    s = mx_kscale(K)[:, None]
    d = mx_kscale(M)[:, None]
    u = mx_kscale(H)[:, None]
    tab_words, tab_scales = pack_weight(n((K, T)) * s, "e4m3")
    tab2_words, tab2_scales = pack_weight(n((K, T)) * s, "e4m3")
    w3_words, w3_scales = pack_weight(n((K, H)) / np.sqrt(K) / s * u.T, "e2m1")
    wr_words, wr_scales = pack_weight(1.8 * n((K, H)) / np.sqrt(K) / s, "e4m3")
    return {
        "tab_words": tab_words, "tab_scales": tab_scales,
        "tab2_words": tab2_words, "tab2_scales": tab2_scales,
        "offs": striped(np.random.permutation(T)[:S]),
        "offs2": striped(np.random.permutation(T)[:S]),
        "offs3": striped(np.random.permutation(T2)[:S]),
        "offs4": striped(np.random.permutation(T2)[:S]),
        "w1": (2.0 * n((K, M)) / np.sqrt(K) / s).astype(np.float32),
        "gain": (np.exp(0.3 * n(M)) * d[:, 0]).astype(np.float32),
        "w2": (1.6 * n((M, H)) / np.sqrt(M) / d * u.T).astype(np.float32),
        "w3_words": w3_words, "w3_scales": w3_scales,
        "wr_words": wr_words, "wr_scales": wr_scales,
        "wg1": np.exp(0.3 * n((128, S))).astype(np.float32),
        "wg2": np.exp(0.3 * n((128, S))).astype(np.float32),
        "clim": (0.5 * n((H, T2)) * u).astype(np.float32),
        "wo": (1.4 * n((H, N)) / np.sqrt(H) / u).astype(np.float32),
    }

def reference(tab_words, tab_scales, tab2_words, tab2_scales, offs, offs2, offs3, offs4, w1, gain, w2, w3_words, w3_scales, wr_words, wr_scales, wg1, wg2, clim, wo):
    v = unpack_weight(tab_words, tab_scales, "e4m3")[:, unstriped(offs)]
    v2 = unpack_weight(tab2_words, tab2_scales, "e4m3")[:, unstriped(offs2)]
    act = np.tanh(mxq(f64(w1), 0, "e4m3").T @ v) * f64(gain)[:, None]
    h1 = mxq(f64(w2), 0, "e4m3").T @ mxq(act, 0, "e4m3") + unpack_weight(w3_words, w3_scales, "e2m1").T @ v
    h2 = np.tanh(unpack_weight(wr_words, wr_scales, "e4m3").T @ v2)
    pa = np.zeros((H, T2))
    pa[:, unstriped(offs3)] = np.tile(f64(wg1), (H // 128, 1)) * h1
    pb = np.zeros((H, T2))
    pb[:, unstriped(offs4)] = np.tile(f64(wg2), (H // 128, 1)) * h2
    z = pa * pb + f64(clim)
    y = mxq(f64(wo), 0, "e4m3").T @ mxq(z, 0, "e4m3")
    return np.abs(y)

@@ -1,0 +1,302 @@
+from contextlib import ExitStack
+
+import concourse.mybir as mybir
+from concourse.masks import make_identity
+
+K, M, H, N, S, T, T2 = 1024, 512, 1024, 512, 512, 2048, 1024
+FLOPS = 2 * S * (K * M + M * H + 2 * K * H) + 2 * H * N * T2
+
+F32 = mybir.dt.float32
+BF16 = mybir.dt.bfloat16
+I32 = mybir.dt.int32
+U32 = mybir.dt.uint32
+U16 = mybir.dt.uint16
+U8 = mybir.dt.uint8
+FP8X4 = mybir.dt.float8_e4m3fn_x4
+FP4X4 = mybir.dt.float4_e2m1fn_x4
+ACT = mybir.ActivationFunctionType
+MULT = mybir.AluOpType.mult
+
+P = 128
+SLICES = H // P
+PA_PAGES = 2
+WR_PIECES = ((0, 2), (2, 5), (5, 8))
+
+
+def tile_list_ice_chart_features_kernel(
+    tc, tab_words, tab_scales, tab2_words, tab2_scales, offs, offs2, offs3, offs4, w1, gain, w2,
+    w3_words, w3_scales, wr_words, wr_scales, wg1, wg2, clim, wo, out,
+):
+    nc = tc.nc
+    with ExitStack() as ctx:
+        keep = ctx.enter_context(tc.tile_pool(name="keep", bufs=1))
+        ring = ctx.enter_context(tc.tile_pool(name="ring", bufs=1))
+        reused = ctx.enter_context(tc.tile_pool(name="reused", bufs=1))
+        psum = ctx.enter_context(tc.psum_pool(name="psum", bufs=1))
+
+        def kept(name, shape, dtype):
+            return keep.tile(shape, dtype, name=name, align_bytes=64)
+
+        def staged(name, shape, dtype):
+            return ring.tile(shape, dtype, name=name, tag="stage", bufs=4, align_bytes=64)
+
+        def bank(name):
+            return psum.tile([P, 512], F32, name=name, tag="mm", bufs=3)
+
+        lists = {}
+
+        def load_list(name, src):
+            lists[name] = kept(name, [P, S // 16], U16)
+            nc.sync.dma_start(lists[name][:], src)
+
+        def load_packed_scales(tile, src):
+            for q in range(4):
+                nc.sync.dma_start(tile[32 * q : 32 * q + 8, :].bitcast(I32), src[:, 4 * q : 4 * q + 4, :].bitcast(I32))
+
+        def load_scales(tile, src):
+            for q in range(4):
+                nc.sync.dma_start(
+                    tile[32 * q : 32 * q + 4, :, :].bitcast(I32),
+                    src[:, 4 * q : 4 * q + 4, :].rearrange("a r c -> r a c").bitcast(I32),
+                )
+
+        def load_table_pass(window, words, a):
+            nc.sync.dma_start(window[:].bitcast(I32), words[a].rearrange("p t i -> p (t i)").bitcast(I32))
+            return window
+
+        def load_rows(name, rows):
+            raw = staged(name, [P, 4, 512], F32)
+            nc.sync.dma_start(raw[:], rows.rearrange("(p j) c -> p j c", j=4))
+            return raw
+
+        wr = {}
+
+        def load_wr(first, last):
+            piece = kept("wr%d" % first, [P, 2, P * (last - first)], U32)
+            src = wr_words.rearrange("a p c i -> p a (c i)")[:, :, 4 * P * first : 4 * P * last]
+            nc.sync.dma_start(piece[:].bitcast(I32), src.bitcast(I32))
+            for s in range(first, last):
+                wr[s] = [piece[:, a, P * (s - first) : P * (s - first + 1)] for a in range(2)]
+
+        def window(name, slot):
+            return reused.tile([P, T], U32, name=name, offset=4 * T * slot)
+
+        def late_pages(name, slot):
+            pages = [
+                reused.tile([P, T2], F32, name="%s%d" % (name, i), offset=4 * T * slot + 4 * T2 * i) for i in range(2)
+            ]
+            for page in pages:
+                nc.gpsimd.memset(page[:].bitcast(I32), 0)
+            return pages
+
+        def load_clim(s):
+            rows = ring.tile([P, T2], F32, name="clim%d" % s, tag="clim", bufs=3)
+            nc.sync.dma_start(rows[:], clim[P * s : P * (s + 1), :])
+            return rows
+
+        tab2_sc = kept("tab2_sc", [P, T], U8)
+        wr_sc = kept("wr_sc", [P, H], U8)
+        tab_sc = kept("tab_sc", [P, 2, T], U8)
+        w3_sc = kept("w3_sc", [P, 2, H], U8)
+        nc.vector.memset(tab2_sc[:].bitcast(I32), 0)
+        nc.vector.memset(wr_sc[:].bitcast(I32), 0)
+        pb_pages = [kept("pb%d" % i, [P, T2], F32) for i in range(2)]
+        for page in pb_pages:
+            nc.vector.memset(page[:].bitcast(I32), 0)
+        nc.gpsimd.memset(tab_sc[:].bitcast(I32), 0)
+        nc.gpsimd.memset(w3_sc[:].bitcast(I32), 0)
+        ident = kept("ident", [P, P], F32)
+        make_identity(nc, ident[:])
+
+        load_list("offs2", offs2)
+        tab2_win = [load_table_pass(window("tab2_0", 0), tab2_words, 0)]
+        load_packed_scales(tab2_sc, tab2_scales)
+        tab2_win.append(load_table_pass(window("tab2_1", 1), tab2_words, 1))
+        load_wr(*WR_PIECES[0])
+        load_packed_scales(wr_sc, wr_scales)
+        load_list("offs4", offs4)
+        wg2_sb = kept("wg2", [P, S], F32)
+        nc.sync.dma_start(wg2_sb[:], wg2)
+        w1_raw = [load_rows("w1_%d" % a, w1[512 * a : 512 * (a + 1), :]) for a in range(2)]
+        load_list("offs", offs)
+        tab_win = [load_table_pass(window("tab_0", 2), tab_words, 0)]
+        load_scales(tab_sc, tab_scales)
+        w2_raw = [load_rows("w2_0", w2[:, 0:512])]
+        tab_win.append(load_table_pass(window("tab_1", 3), tab_words, 1))
+        load_wr(*WR_PIECES[1])
+        gain_sb = kept("gain", [P, 4], F32)
+        nc.sync.dma_start(gain_sb[:], gain.rearrange("(p t) -> p t", t=4))
+        load_scales(w3_sc, w3_scales)
+        w3 = kept("w3", [P, 2, 2 * H], U8)
+        nc.sync.dma_start(w3[:].bitcast(I32), w3_words.rearrange("a p c -> p a c").bitcast(I32))
+        load_list("offs3", offs3)
+        wg1_sb = kept("wg1", [P, S], F32)
+        nc.sync.dma_start(wg1_sb[:], wg1)
+        load_wr(*WR_PIECES[2])
+        clim_sb = [load_clim(0), load_clim(1)]
+        w2_raw.append(load_rows("w2_1", w2[:, 512:1024]))
+        clim_sb.append(load_clim(2))
+        wo_raw = [load_rows("wo_%d" % g, wo[512 * g : 512 * (g + 1), :]) for g in range(2)]
+        clim_sb.extend([load_clim(s) for s in range(3, SLICES)])
+
+        def gather(name, window, list_name, dtype):
+            picked = kept(name, [P, S], dtype)
+            nc.vector.tensor_copy(picked[:], window.indirect(lists[list_name][:]))
+            return picked
+
+        def grouped_tile(name):
+            return ring.tile([P, 2048], BF16, name=name, tag="grouped", bufs=3, align_bytes=64)
+
+        def interleave(name, rows):
+            grouped = grouped_tile(name)
+            nc.scalar.copy(
+                grouped[:].rearrange("p (c i j) -> p c j i", i=4, j=4),
+                rows.rearrange("p j (c i) -> p c j i", i=4),
+            )
+            return grouped
+
+        def quantise(name, grouped):
+            codes = kept(name + "_codes", [P, 512], U32)
+            scales = kept(name + "_scales", [P, 512], U8)
+            nc.vector.quantize_mx(codes[:].bitcast(FP8X4), scales[:], grouped[:])
+            return codes, scales
+
+        def place_pb(s, h2):
+            acc = bank("h2_acc%d" % s)
+            for a in range(2):
+                nc.tensor.matmul_mx(
+                    acc[:], wr[s][a].bitcast(FP8X4), wr_sc[4 * a :, P * s : P * (s + 1)],
+                    v2[a][:].bitcast(FP8X4), v2_sc[4 * a :, :], start=(a == 0), stop=(a == 1),
+                )
+            nc.scalar.activation(h2[:], acc[:], ACT.Tanh)
+            nc.vector.tensor_tensor(pb_pages[s][:].indirect(lists["offs4"][:]), h2[:], wg2_sb[:], MULT)
+
+        def h2_tile(s):
+            return ring.tile([P, S], F32, name="h2_%d" % s, tag="h2", bufs=3)
+
+        def place_pa(s):
+            acc = bank("h1_acc%d" % s)
+            for a in range(2):
+                nc.tensor.matmul_mx(
+                    acc[:], w3[:, a, 2 * P * s : 2 * P * (s + 1)].bitcast(FP4X4), w3_sc[:, a, P * s : P * (s + 1)],
+                    v[a][:].bitcast(FP8X4), v_sc[a][:], start=(a == 0), stop=False,
+                )
+            codes, scales = w2_q[s // 4]
+            cols = slice(P * (s % 4), P * (s % 4 + 1))
+            nc.tensor.matmul_mx(
+                acc[:], codes[:, cols].bitcast(FP8X4), scales[:, cols], act_q[0][:].bitcast(FP8X4), act_q[1][:],
+                start=False, stop=True,
+            )
+            h1 = ring.tile([P, S], F32, name="h1_%d" % s, tag="h1", bufs=3)
+            nc.scalar.copy(h1[:], acc[:])
+            nc.vector.tensor_tensor(pa_pages[s % PA_PAGES][:].indirect(lists["offs3"][:]), h1[:], wg1_sb[:], MULT)
+
+        z_t = [[kept("z_t%d%d" % (g, half), [P, 4, 2, 256], BF16) for half in range(2)] for g in range(2)]
+        z_codes = [kept("z_codes%d" % g, [P, T2], U32) for g in range(2)]
+        z_scales = [kept("z_scales%d" % g, [P, T2], U8) for g in range(2)]
+
+        def turn_z_rows(s):
+            for half in range(2):
+                cells = slice(512 * half, 512 * (half + 1))
+                prod = ring.tile([P, 512], F32, name="prod%d%d" % (s, half), tag="prod", bufs=4)
+                nc.vector.tensor_tensor(
+                    prod[:], pa_pages[s % PA_PAGES][:, cells], pb_pages[s][:, cells], MULT
+                )
+                turned = psum.tile([P, 4, P], F32, name="turned%d%d" % (s, half), tag="turned", bufs=3)
+                for c in range(4):
+                    first = 512 * half + P * c
+                    nc.tensor.matmul(
+                        turned[:, c, :], clim_sb[s][:, first : first + P], ident[:],
+                        start=(c == 0), stop=False, is_transpose=True,
+                    )
+                for c in range(4):
+                    nc.tensor.matmul(
+                        turned[:, c, :], prod[:, P * c : P * (c + 1)], ident[:],
+                        start=False, stop=(c == 3), is_transpose=True,
+                    )
+                place = slice(64 * (s % 4), 64 * (s % 4 + 1))
+                nc.scalar.copy(
+                    z_t[s // 4][half][:, :, :, place].rearrange("p c u (q e) -> p c u q e", e=2),
+                    turned[:].rearrange("p c (q u e) -> p c u q e", u=2, e=2),
+                )
+
+        def quantise_z(g, pair, copy_out):
+            back = psum.tile([P, 2, 2, P], F32, name="back%d%d" % (g, pair), tag="back", bufs=2)
+            words = z_t[g][pair // 2][:].bitcast(F32)
+            for c in range(2):
+                for u in range(2):
+                    nc.tensor.transpose(back[:, c, u, :], words[:, 2 * (pair % 2) + c, u, :], ident[:])
+            grouped = ring.tile([P, 1024], BF16, name="z_grouped%d%d" % (g, pair), tag="z_grouped", bufs=4, align_bytes=64)
+            copy_out(
+                grouped[:].bitcast(F32).rearrange("p (c r u) -> p c r u", c=2, u=2),
+                back[:].rearrange("p c u r -> p c r u"),
+            )
+            cells = slice(256 * pair, 256 * (pair + 1))
+            nc.vector.quantize_mx(z_codes[g][:, cells].bitcast(FP8X4), z_scales[g][:, cells], grouped[:])
+
+        v2 = [gather("v2_0", tab2_win[0][:], "offs2", U32)]
+        v2_sc = gather("v2_sc", tab2_sc[:], "offs2", U8)
+        v2.append(gather("v2_1", tab2_win[1][:], "offs2", U32))
+        pb_pages.extend(late_pages("pb_a", 0) + late_pages("pb_b", 1))
+        place_pb(0, h2_tile(0))
+        place_pb(1, h2_tile(1))
+
+        w1_q = []
+        for a in range(2):
+            grouped = grouped_tile("w1_grouped%d" % a)
+            nc.scalar.copy(
+                grouped[:].rearrange("p (t q j) -> p q j t", t=4, j=4),
+                w1_raw[a][:].rearrange("p j (q t) -> p q j t", t=4),
+            )
+            w1_q.append(quantise("w1_%d" % a, grouped))
+        v = [gather("v_0", tab_win[0][:], "offs", U32)]
+        v_sc = [gather("v_sc%d" % a, tab_sc[:, a, :], "offs", U8) for a in range(2)]
+        v.append(gather("v_1", tab_win[1][:], "offs", U32))
+        pb_pages.extend(late_pages("pb_c", 2))
+        pa_pages = late_pages("pa", 3)
+        w2_q = [quantise("w2_0", interleave("w2_grouped0", w2_raw[0][:]))]
+        for s in range(2, 5):
+            place_pb(s, h2_tile(s))
+        act_rows = reused.tile([P, 4, S], BF16, name="act_rows", offset=16 * T)
+        for t in range(4):
+            acc = bank("act_acc%d" % t)
+            cols = slice(P * t, P * (t + 1))
+            for a in range(2):
+                nc.tensor.matmul_mx(
+                    acc[:], w1_q[a][0][:, cols].bitcast(FP8X4), w1_q[a][1][:, cols],
+                    v[a][:].bitcast(FP8X4), v_sc[a][:], start=(a == 0), stop=(a == 1),
+                )
+            squashed = ring.tile([P, S], F32, name="squashed%d" % t, tag="squashed", bufs=2)
+            nc.scalar.activation(squashed[:], acc[:], ACT.Tanh)
+            nc.scalar.activation(act_rows[:, t, :], squashed[:], ACT.Copy, scale=gain_sb[:, t : t + 1])
+        act_grouped = interleave("act_grouped", act_rows[:])
+        act_q = quantise("act", act_grouped)
+        for s in range(5, SLICES):
+            place_pb(s, reused.tile([P, S], F32, name="h2_%d" % s, offset=16 * T + 4 * S * (s % 2)))
+        w2_q.append(quantise("w2_1", interleave("w2_grouped1", w2_raw[1][:])))
+
+        place_pa(0)
+        for s in range(SLICES):
+            if s + 1 < SLICES:
+                place_pa(s + 1)
+            turn_z_rows(s)
+            if s == 3:
+                for pair in range(4):
+                    quantise_z(0, pair, nc.scalar.copy)
+        wo_q = [quantise("wo_%d" % g, interleave("wo_grouped%d" % g, wo_raw[g][:])) for g in range(2)]
+
+        for pair in range(4):
+            quantise_z(1, pair, nc.vector.tensor_copy)
+            cells = slice(256 * pair, 256 * (pair + 1))
+            for n0 in range(0, N // P, 2):
+                acc = bank("y_acc%d%d" % (pair, n0))
+                for i in range(2):
+                    cols = slice(P * (n0 + i), P * (n0 + i + 1))
+                    for g in range(2):
+                        nc.tensor.matmul_mx(
+                            acc[:, 256 * i : 256 * (i + 1)], wo_q[g][0][:, cols].bitcast(FP8X4), wo_q[g][1][:, cols],
+                            z_codes[g][:, cells].bitcast(FP8X4), z_scales[g][:, cells], start=(g == 0), stop=(g == 1),
+                        )
+                result = ring.tile([P, 2, 256], F32, name="result%d%d" % (pair, n0), tag="result", bufs=4)
+                nc.scalar.activation(result[:], acc[:].rearrange("p (i c) -> p i c", i=2), ACT.Abs)
+                nc.sync.dma_start(out[P * n0 : P * (n0 + 2), cells].rearrange("(i p) c -> p i c", i=2), result[:])

@@ -19,7 +19,8 @@ MULT = mybir.AluOpType.mult
 
 P = 128
 SLICES = H // P
-PA_PAGES = 2
+PA_PAGES = 3
+LAST_BYTES = 16 * T + 8 * S
 WR_PIECES = ((0, 2), (2, 5), (5, 8))
 
 
@@ -96,7 +97,8 @@ def tile_list_ice_chart_features_kernel(
 
         tab2_sc = kept("tab2_sc", [P, T], U8)
         wr_sc = kept("wr_sc", [P, H], U8)
-        tab_sc = kept("tab_sc", [P, 2, T], U8)
+        tab_sc = kept("tab_sc", [P, T], U8)
+        v_sc1 = kept("v_sc1", [P, S], U8)
         w3_sc = kept("w3_sc", [P, 2, H], U8)
         nc.vector.memset(tab2_sc[:].bitcast(I32), 0)
         nc.vector.memset(wr_sc[:].bitcast(I32), 0)
@@ -105,6 +107,9 @@ def tile_list_ice_chart_features_kernel(
             nc.vector.memset(page[:].bitcast(I32), 0)
         nc.gpsimd.memset(tab_sc[:].bitcast(I32), 0)
         nc.gpsimd.memset(w3_sc[:].bitcast(I32), 0)
+        nc.gpsimd.memset(v_sc1[:].bitcast(I32), 0)
+        pa_pages = [kept("pa_early", [P, T2], F32)]
+        nc.gpsimd.memset(pa_pages[0][:].bitcast(I32), 0)
         ident = kept("ident", [P, P], F32)
         make_identity(nc, ident[:])
 
@@ -120,7 +125,7 @@ def tile_list_ice_chart_features_kernel(
         w1_raw = [load_rows("w1_%d" % a, w1[512 * a : 512 * (a + 1), :]) for a in range(2)]
         load_list("offs", offs)
         tab_win = [load_table_pass(window("tab_0", 2), tab_words, 0)]
-        load_scales(tab_sc, tab_scales)
+        load_packed_scales(tab_sc, tab_scales)
         w2_raw = [load_rows("w2_0", w2[:, 0:512])]
         tab_win.append(load_table_pass(window("tab_1", 3), tab_words, 1))
         load_wr(*WR_PIECES[1])
@@ -145,15 +150,13 @@ def tile_list_ice_chart_features_kernel(
             return picked
 
         def grouped_tile(name):
-            return ring.tile([P, 2048], BF16, name=name, tag="grouped", bufs=3, align_bytes=64)
+            return ring.tile([P, 2048], BF16, name=name, tag="grouped", bufs=2, align_bytes=64)
 
-        def interleave(name, rows):
-            grouped = grouped_tile(name)
+        def interleave(grouped, rows):
             nc.scalar.copy(
-                grouped[:].rearrange("p (c i j) -> p c j i", i=4, j=4),
+                grouped.rearrange("p (c i j) -> p c j i", i=4, j=4),
                 rows.rearrange("p j (c i) -> p c j i", i=4),
             )
-            return grouped
 
         def quantise(name, grouped):
             codes = kept(name + "_codes", [P, 512], U32)
@@ -161,15 +164,19 @@ def tile_list_ice_chart_features_kernel(
             nc.vector.quantize_mx(codes[:].bitcast(FP8X4), scales[:], grouped[:])
             return codes, scales
 
-        def place_pb(s, h2):
-            acc = bank("h2_acc%d" % s)
-            for a in range(2):
-                nc.tensor.matmul_mx(
-                    acc[:], wr[s][a].bitcast(FP8X4), wr_sc[4 * a :, P * s : P * (s + 1)],
-                    v2[a][:].bitcast(FP8X4), v2_sc[4 * a :, :], start=(a == 0), stop=(a == 1),
-                )
-            nc.scalar.activation(h2[:], acc[:], ACT.Tanh)
-            nc.vector.tensor_tensor(pb_pages[s][:].indirect(lists["offs4"][:]), h2[:], wg2_sb[:], MULT)
+        def place_pb(s, h2, parts=1):
+            width = S // parts
+            for i in range(parts):
+                picks = slice(width * i, width * (i + 1))
+                acc = bank("h2_acc%d%d" % (s, i))
+                for a in range(2):
+                    nc.tensor.matmul_mx(
+                        acc[:, :width], wr[s][a].bitcast(FP8X4), wr_sc[4 * a :, P * s : P * (s + 1)],
+                        v2[a][:, picks].bitcast(FP8X4), v2_sc[4 * a :, picks], start=(a == 0), stop=(a == 1),
+                    )
+                nc.scalar.activation(h2[:, picks], acc[:, :width], ACT.Tanh)
+                offsets = lists["offs4"][:, width // 16 * i : width // 16 * (i + 1)]
+                nc.vector.tensor_tensor(pb_pages[s][:].indirect(offsets), h2[:, picks], wg2_sb[:, picks], MULT)
 
         def h2_tile(s):
             return ring.tile([P, S], F32, name="h2_%d" % s, tag="h2", bufs=3)
@@ -179,7 +186,7 @@ def tile_list_ice_chart_features_kernel(
             for a in range(2):
                 nc.tensor.matmul_mx(
                     acc[:], w3[:, a, 2 * P * s : 2 * P * (s + 1)].bitcast(FP4X4), w3_sc[:, a, P * s : P * (s + 1)],
-                    v[a][:].bitcast(FP8X4), v_sc[a][:], start=(a == 0), stop=False,
+                    v[a][:].bitcast(FP8X4), (v_sc, v_sc1)[a][:], start=(a == 0), stop=False,
                 )
             codes, scales = w2_q[s // 4]
             cols = slice(P * (s % 4), P * (s % 4 + 1))
@@ -187,21 +194,33 @@ def tile_list_ice_chart_features_kernel(
                 acc[:], codes[:, cols].bitcast(FP8X4), scales[:, cols], act_q[0][:].bitcast(FP8X4), act_q[1][:],
                 start=False, stop=True,
             )
-            h1 = ring.tile([P, S], F32, name="h1_%d" % s, tag="h1", bufs=3)
-            nc.scalar.copy(h1[:], acc[:])
-            nc.vector.tensor_tensor(pa_pages[s % PA_PAGES][:].indirect(lists["offs3"][:]), h1[:], wg1_sb[:], MULT)
+            if s + 1 < SLICES:
+                weighted = ring.tile([P, S], F32, name="weighted%d" % s, tag="weighted", bufs=2)
+            else:
+                weighted = reused.tile([P, S], F32, name="weighted%d" % s, offset=LAST_BYTES)
+            if s < 2:
+                nc.vector.tensor_tensor(weighted[:], acc[:], wg1_sb[:], MULT)
+            else:
+                h1 = ring.tile([P, S], F32, name="h1_%d" % s, tag="h1", bufs=2)
+                nc.scalar.copy(h1[:], acc[:])
+                nc.gpsimd.tensor_tensor(weighted[:], h1[:], wg1_sb[:], MULT)
+            nc.vector.tensor_copy(pa_pages[s % PA_PAGES][:].indirect(lists["offs3"][:]), weighted[:])
 
         z_t = [[kept("z_t%d%d" % (g, half), [P, 4, 2, 256], BF16) for half in range(2)] for g in range(2)]
         z_codes = [kept("z_codes%d" % g, [P, T2], U32) for g in range(2)]
-        z_scales = [kept("z_scales%d" % g, [P, T2], U8) for g in range(2)]
 
         def turn_z_rows(s):
+            pa, pb = pa_pages[s % PA_PAGES], pb_pages[s]
+            if s + 1 < SLICES:
+                whole = ring.tile([P, T2], F32, name="prod%d" % s, tag="prod", bufs=3)
+                nc.gpsimd.tensor_tensor(whole[:], pa[:], pb[:], MULT)
             for half in range(2):
                 cells = slice(512 * half, 512 * (half + 1))
-                prod = ring.tile([P, 512], F32, name="prod%d%d" % (s, half), tag="prod", bufs=4)
-                nc.vector.tensor_tensor(
-                    prod[:], pa_pages[s % PA_PAGES][:, cells], pb_pages[s][:, cells], MULT
-                )
+                if s + 1 < SLICES:
+                    prod = whole[:, cells]
+                else:
+                    prod = ring.tile([P, 512], F32, name="prod%d%d" % (s, half), tag="prod", bufs=3)
+                    nc.vector.tensor_tensor(prod[:], pa[:, cells], pb[:, cells], MULT)
                 turned = psum.tile([P, 4, P], F32, name="turned%d%d" % (s, half), tag="turned", bufs=3)
                 for c in range(4):
                     first = 512 * half + P * c
@@ -220,25 +239,26 @@ def tile_list_ice_chart_features_kernel(
                     turned[:].rearrange("p c (q u e) -> p c u q e", u=2, e=2),
                 )
 
-        def quantise_z(g, pair, copy_out):
+        def turn_z_back(g, pair, grouped, copy_out):
             back = psum.tile([P, 2, 2, P], F32, name="back%d%d" % (g, pair), tag="back", bufs=2)
             words = z_t[g][pair // 2][:].bitcast(F32)
             for c in range(2):
                 for u in range(2):
                     nc.tensor.transpose(back[:, c, u, :], words[:, 2 * (pair % 2) + c, u, :], ident[:])
-            grouped = ring.tile([P, 1024], BF16, name="z_grouped%d%d" % (g, pair), tag="z_grouped", bufs=4, align_bytes=64)
             copy_out(
-                grouped[:].bitcast(F32).rearrange("p (c r u) -> p c r u", c=2, u=2),
+                grouped.bitcast(F32).rearrange("p (c r u) -> p c r u", c=2, u=2),
                 back[:].rearrange("p c u r -> p c r u"),
             )
-            cells = slice(256 * pair, 256 * (pair + 1))
-            nc.vector.quantize_mx(z_codes[g][:, cells].bitcast(FP8X4), z_scales[g][:, cells], grouped[:])
 
         v2 = [gather("v2_0", tab2_win[0][:], "offs2", U32)]
         v2_sc = gather("v2_sc", tab2_sc[:], "offs2", U8)
-        v2.append(gather("v2_1", tab2_win[1][:], "offs2", U32))
+        v2.append(kept("v2_1", [P, S], U32))
+        for i in range(2):
+            nc.vector.tensor_copy(
+                v2[1][:, 256 * i : 256 * (i + 1)], tab2_win[1][:].indirect(lists["offs2"][:, 16 * i : 16 * (i + 1)])
+            )
         pb_pages.extend(late_pages("pb_a", 0) + late_pages("pb_b", 1))
-        place_pb(0, h2_tile(0))
+        place_pb(0, h2_tile(0), parts=2)
         place_pb(1, h2_tile(1))
 
         w1_q = []
@@ -250,11 +270,15 @@ def tile_list_ice_chart_features_kernel(
             )
             w1_q.append(quantise("w1_%d" % a, grouped))
         v = [gather("v_0", tab_win[0][:], "offs", U32)]
-        v_sc = [gather("v_sc%d" % a, tab_sc[:, a, :], "offs", U8) for a in range(2)]
+        v_sc = gather("v_sc", tab_sc[:], "offs", U8)
+        for q in range(4):
+            nc.gpsimd.dma_start(v_sc1[32 * q : 32 * q + 4, :].bitcast(I32), v_sc[32 * q + 4 : 32 * q + 8, :].bitcast(I32))
         v.append(gather("v_1", tab_win[1][:], "offs", U32))
         pb_pages.extend(late_pages("pb_c", 2))
-        pa_pages = late_pages("pa", 3)
-        w2_q = [quantise("w2_0", interleave("w2_grouped0", w2_raw[0][:]))]
+        pa_pages.extend(late_pages("pa", 3))
+        w2_grouped = grouped_tile("w2_grouped0")
+        interleave(w2_grouped[:], w2_raw[0][:])
+        w2_q = [quantise("w2_0", w2_grouped)]
         for s in range(2, 5):
             place_pb(s, h2_tile(s))
         act_rows = reused.tile([P, 4, S], BF16, name="act_rows", offset=16 * T)
@@ -264,37 +288,58 @@ def tile_list_ice_chart_features_kernel(
             for a in range(2):
                 nc.tensor.matmul_mx(
                     acc[:], w1_q[a][0][:, cols].bitcast(FP8X4), w1_q[a][1][:, cols],
-                    v[a][:].bitcast(FP8X4), v_sc[a][:], start=(a == 0), stop=(a == 1),
+                    v[a][:].bitcast(FP8X4), v_sc[4 * a :, :], start=(a == 0), stop=(a == 1),
                 )
             squashed = ring.tile([P, S], F32, name="squashed%d" % t, tag="squashed", bufs=2)
             nc.scalar.activation(squashed[:], acc[:], ACT.Tanh)
             nc.scalar.activation(act_rows[:, t, :], squashed[:], ACT.Copy, scale=gain_sb[:, t : t + 1])
-        act_grouped = interleave("act_grouped", act_rows[:])
+        act_grouped = grouped_tile("act_grouped")
+        interleave(act_grouped[:], act_rows[:])
         act_q = quantise("act", act_grouped)
         for s in range(5, SLICES):
             place_pb(s, reused.tile([P, S], F32, name="h2_%d" % s, offset=16 * T + 4 * S * (s % 2)))
-        w2_q.append(quantise("w2_1", interleave("w2_grouped1", w2_raw[1][:])))
+        w2_grouped = grouped_tile("w2_grouped1")
+        interleave(w2_grouped[:], w2_raw[1][:])
+        w2_q.append(quantise("w2_1", w2_grouped))
 
+        wo_grouped = staged("wo_grouped", [P, 2, 2048], BF16)
+        z0_grouped = staged("z0_grouped", [P, 4, 1024], BF16)
         place_pa(0)
+        place_pa(1)
         for s in range(SLICES):
-            if s + 1 < SLICES:
-                place_pa(s + 1)
+            if s + 2 < SLICES:
+                place_pa(s + 2)
             turn_z_rows(s)
+            if s < 2:
+                interleave(wo_grouped[:, s, :], wo_raw[s][:])
             if s == 3:
                 for pair in range(4):
-                    quantise_z(0, pair, nc.scalar.copy)
-        wo_q = [quantise("wo_%d" % g, interleave("wo_grouped%d" % g, wo_raw[g][:])) for g in range(2)]
+                    turn_z_back(0, pair, z0_grouped[:, pair, :], nc.scalar.copy)
+        z_scales = [
+            reused.tile([P, T2], U8, name="z_scales0", offset=LAST_BYTES, align_bytes=64),
+            kept("z_scales1", [P, T2], U8),
+        ]
+        nc.vector.quantize_mx(z_codes[0][:].bitcast(FP8X4), z_scales[0][:], z0_grouped[:].rearrange("p a c -> p (a c)"))
+        wo_codes = kept("wo_codes", [P, 2, N], U32)
+        wo_scales = reused.tile([P, 2, N], U8, name="wo_scales", offset=LAST_BYTES + T2, align_bytes=64)
+        nc.vector.quantize_mx(
+            wo_codes[:].rearrange("p g n -> p (g n)").bitcast(FP8X4),
+            wo_scales[:].rearrange("p g n -> p (g n)"),
+            wo_grouped[:].rearrange("p g c -> p (g c)"),
+        )
 
         for pair in range(4):
-            quantise_z(1, pair, nc.vector.tensor_copy)
             cells = slice(256 * pair, 256 * (pair + 1))
+            grouped = ring.tile([P, 1024], BF16, name="z_grouped%d" % pair, tag="z_grouped", bufs=2, align_bytes=64)
+            turn_z_back(1, pair, grouped[:], nc.scalar.copy if pair == 0 else nc.vector.tensor_copy)
+            nc.vector.quantize_mx(z_codes[1][:, cells].bitcast(FP8X4), z_scales[1][:, cells], grouped[:])
             for n0 in range(0, N // P, 2):
                 acc = bank("y_acc%d%d" % (pair, n0))
                 for i in range(2):
                     cols = slice(P * (n0 + i), P * (n0 + i + 1))
                     for g in range(2):
                         nc.tensor.matmul_mx(
-                            acc[:, 256 * i : 256 * (i + 1)], wo_q[g][0][:, cols].bitcast(FP8X4), wo_q[g][1][:, cols],
+                            acc[:, 256 * i : 256 * (i + 1)], wo_codes[:, g, cols].bitcast(FP8X4), wo_scales[:, g, cols],
                             z_codes[g][:, cells].bitcast(FP8X4), z_scales[g][:, cells], start=(g == 0), stop=(g == 1),
                         )
                 result = ring.tile([P, 2, 256], F32, name="result%d%d" % (pair, n0), tag="result", bufs=4)

@@ -21,7 +21,9 @@ P = 128
 SLICES = H // P
 PA_PAGES = 3
 LAST_BYTES = 16 * T + 8 * S
-WR_PIECES = ((0, 2), (2, 5), (5, 8))
+WO_BYTES = LAST_BYTES + 4 * S
+WEIGHTED_ON_GPSIMD = (3, 4)
+WR_PIECES = ((0, 2), (2, 8))
 
 
 def tile_list_ice_chart_features_kernel(
@@ -42,7 +44,7 @@ def tile_list_ice_chart_features_kernel(
             return ring.tile(shape, dtype, name=name, tag="stage", bufs=4, align_bytes=64)
 
         def bank(name):
-            return psum.tile([P, 512], F32, name=name, tag="mm", bufs=3)
+            return psum.tile([P, 512], F32, name=name, tag="mm", bufs=4)
 
         lists = {}
 
@@ -131,18 +133,15 @@ def tile_list_ice_chart_features_kernel(
         load_wr(*WR_PIECES[1])
         gain_sb = kept("gain", [P, 4], F32)
         nc.sync.dma_start(gain_sb[:], gain.rearrange("(p t) -> p t", t=4))
+        w2_raw.append(load_rows("w2_1", w2[:, 512:1024]))
         load_scales(w3_sc, w3_scales)
         w3 = kept("w3", [P, 2, 2 * H], U8)
         nc.sync.dma_start(w3[:].bitcast(I32), w3_words.rearrange("a p c -> p a c").bitcast(I32))
         load_list("offs3", offs3)
         wg1_sb = kept("wg1", [P, S], F32)
         nc.sync.dma_start(wg1_sb[:], wg1)
-        load_wr(*WR_PIECES[2])
-        clim_sb = [load_clim(0), load_clim(1)]
-        w2_raw.append(load_rows("w2_1", w2[:, 512:1024]))
-        clim_sb.append(load_clim(2))
         wo_raw = [load_rows("wo_%d" % g, wo[512 * g : 512 * (g + 1), :]) for g in range(2)]
-        clim_sb.extend([load_clim(s) for s in range(3, SLICES)])
+        clim_sb = [load_clim(s) for s in range(SLICES)]
 
         def gather(name, window, list_name, dtype):
             picked = kept(name, [P, S], dtype)
@@ -150,7 +149,7 @@ def tile_list_ice_chart_features_kernel(
             return picked
 
         def grouped_tile(name):
-            return ring.tile([P, 2048], BF16, name=name, tag="grouped", bufs=2, align_bytes=64)
+            return ring.tile([P, 2048], BF16, name=name, tag="grouped", bufs=3, align_bytes=64)
 
         def interleave(grouped, rows):
             nc.scalar.copy(
@@ -179,7 +178,7 @@ def tile_list_ice_chart_features_kernel(
                 nc.vector.tensor_tensor(pb_pages[s][:].indirect(offsets), h2[:, picks], wg2_sb[:, picks], MULT)
 
         def h2_tile(s):
-            return ring.tile([P, S], F32, name="h2_%d" % s, tag="h2", bufs=3)
+            return ring.tile([P, S], F32, name="h2_%d" % s, tag="h2", bufs=5)
 
         def place_pa(s):
             acc = bank("h1_acc%d" % s)
@@ -194,11 +193,13 @@ def tile_list_ice_chart_features_kernel(
                 acc[:], codes[:, cols].bitcast(FP8X4), scales[:, cols], act_q[0][:].bitcast(FP8X4), act_q[1][:],
                 start=False, stop=True,
             )
-            if s + 1 < SLICES:
-                weighted = ring.tile([P, S], F32, name="weighted%d" % s, tag="weighted", bufs=2)
-            else:
+            if s == 0:
+                weighted = reused.tile([P, S], F32, name="weighted0", offset=WO_BYTES)
+            elif s == SLICES - 1:
                 weighted = reused.tile([P, S], F32, name="weighted%d" % s, offset=LAST_BYTES)
-            if s < 2:
+            else:
+                weighted = ring.tile([P, S], F32, name="weighted%d" % s, tag="weighted", bufs=3)
+            if s not in WEIGHTED_ON_GPSIMD:
                 nc.vector.tensor_tensor(weighted[:], acc[:], wg1_sb[:], MULT)
             else:
                 h1 = ring.tile([P, S], F32, name="h1_%d" % s, tag="h1", bufs=2)
@@ -221,7 +222,7 @@ def tile_list_ice_chart_features_kernel(
                 else:
                     prod = ring.tile([P, 512], F32, name="prod%d%d" % (s, half), tag="prod", bufs=3)
                     nc.vector.tensor_tensor(prod[:], pa[:, cells], pb[:, cells], MULT)
-                turned = psum.tile([P, 4, P], F32, name="turned%d%d" % (s, half), tag="turned", bufs=3)
+                turned = psum.tile([P, 4, P], F32, name="turned%d%d" % (s, half), tag="turned", bufs=2)
                 for c in range(4):
                     first = 512 * half + P * c
                     nc.tensor.matmul(
@@ -272,14 +273,14 @@ def tile_list_ice_chart_features_kernel(
         v = [gather("v_0", tab_win[0][:], "offs", U32)]
         v_sc = gather("v_sc", tab_sc[:], "offs", U8)
         for q in range(4):
-            nc.gpsimd.dma_start(v_sc1[32 * q : 32 * q + 4, :].bitcast(I32), v_sc[32 * q + 4 : 32 * q + 8, :].bitcast(I32))
+            nc.sync.dma_start(v_sc1[32 * q : 32 * q + 4, :].bitcast(I32), v_sc[32 * q + 4 : 32 * q + 8, :].bitcast(I32))
         v.append(gather("v_1", tab_win[1][:], "offs", U32))
         pb_pages.extend(late_pages("pb_c", 2))
         pa_pages.extend(late_pages("pa", 3))
         w2_grouped = grouped_tile("w2_grouped0")
         interleave(w2_grouped[:], w2_raw[0][:])
         w2_q = [quantise("w2_0", w2_grouped)]
-        for s in range(2, 5):
+        for s in range(2, SLICES - 1):
             place_pb(s, h2_tile(s))
         act_rows = reused.tile([P, 4, S], BF16, name="act_rows", offset=16 * T)
         for t in range(4):
@@ -295,23 +296,29 @@ def tile_list_ice_chart_features_kernel(
             nc.scalar.activation(act_rows[:, t, :], squashed[:], ACT.Copy, scale=gain_sb[:, t : t + 1])
         act_grouped = grouped_tile("act_grouped")
         interleave(act_grouped[:], act_rows[:])
-        act_q = quantise("act", act_grouped)
-        for s in range(5, SLICES):
-            place_pb(s, reused.tile([P, S], F32, name="h2_%d" % s, offset=16 * T + 4 * S * (s % 2)))
         w2_grouped = grouped_tile("w2_grouped1")
         interleave(w2_grouped[:], w2_raw[1][:])
         w2_q.append(quantise("w2_1", w2_grouped))
+        act_q = quantise("act", act_grouped)
+        place_pb(SLICES - 1, reused.tile([P, S], F32, name="h2_last", offset=16 * T))
 
-        wo_grouped = staged("wo_grouped", [P, 2, 2048], BF16)
+        wo_grouped = reused.tile([P, 2, 2048], BF16, name="wo_grouped", offset=WO_BYTES, align_bytes=64)
         z0_grouped = staged("z0_grouped", [P, 4, 1024], BF16)
+        wo_codes = kept("wo_codes", [P, 2, N], U32)
+        for g in range(2):
+            interleave(wo_grouped[:, g, :], wo_raw[g][:])
+        wo_scales = kept("wo_scales", [P, 2, N], U8)
+        nc.vector.quantize_mx(
+            wo_codes[:].rearrange("p g n -> p (g n)").bitcast(FP8X4),
+            wo_scales[:].rearrange("p g n -> p (g n)"),
+            wo_grouped[:].rearrange("p g c -> p (g c)"),
+        )
         place_pa(0)
         place_pa(1)
         for s in range(SLICES):
             if s + 2 < SLICES:
                 place_pa(s + 2)
             turn_z_rows(s)
-            if s < 2:
-                interleave(wo_grouped[:, s, :], wo_raw[s][:])
             if s == 3:
                 for pair in range(4):
                     turn_z_back(0, pair, z0_grouped[:, pair, :], nc.scalar.copy)
@@ -320,28 +327,23 @@ def tile_list_ice_chart_features_kernel(
             kept("z_scales1", [P, T2], U8),
         ]
         nc.vector.quantize_mx(z_codes[0][:].bitcast(FP8X4), z_scales[0][:], z0_grouped[:].rearrange("p a c -> p (a c)"))
-        wo_codes = kept("wo_codes", [P, 2, N], U32)
-        wo_scales = reused.tile([P, 2, N], U8, name="wo_scales", offset=LAST_BYTES + T2, align_bytes=64)
-        nc.vector.quantize_mx(
-            wo_codes[:].rearrange("p g n -> p (g n)").bitcast(FP8X4),
-            wo_scales[:].rearrange("p g n -> p (g n)"),
-            wo_grouped[:].rearrange("p g c -> p (g c)"),
-        )
 
         for pair in range(4):
             cells = slice(256 * pair, 256 * (pair + 1))
-            grouped = ring.tile([P, 1024], BF16, name="z_grouped%d" % pair, tag="z_grouped", bufs=2, align_bytes=64)
-            turn_z_back(1, pair, grouped[:], nc.scalar.copy if pair == 0 else nc.vector.tensor_copy)
+            grouped = ring.tile([P, 1024], BF16, name="z_grouped%d" % pair, tag="z_grouped", bufs=3, align_bytes=64)
+            turn_z_back(1, pair, grouped[:], nc.scalar.copy if pair == 1 else nc.vector.tensor_copy)
             nc.vector.quantize_mx(z_codes[1][:, cells].bitcast(FP8X4), z_scales[1][:, cells], grouped[:])
+        for pair in range(4):
+            cells = slice(256 * pair, 256 * (pair + 1))
             for n0 in range(0, N // P, 2):
                 acc = bank("y_acc%d%d" % (pair, n0))
-                for i in range(2):
-                    cols = slice(P * (n0 + i), P * (n0 + i + 1))
-                    for g in range(2):
+                for g in range(2):
+                    for i in range(2):
+                        cols = slice(P * (n0 + i), P * (n0 + i + 1))
                         nc.tensor.matmul_mx(
                             acc[:, 256 * i : 256 * (i + 1)], wo_codes[:, g, cols].bitcast(FP8X4), wo_scales[:, g, cols],
-                            z_codes[g][:, cells].bitcast(FP8X4), z_scales[g][:, cells], start=(g == 0), stop=(g == 1),
+                            z_codes[g][:, cells].bitcast(FP8X4), z_scales[g][:, cells], start=(g + i == 0), stop=(g + i == 2),
                         )
-                result = ring.tile([P, 2, 256], F32, name="result%d%d" % (pair, n0), tag="result", bufs=4)
+                result = reused.tile([P, 2, 256], F32, name="result%d%d" % (pair, n0), offset=2048 * (2 * pair + n0 // 2))
                 nc.scalar.activation(result[:], acc[:].rearrange("p (i c) -> p i c", i=2), ACT.Abs)
                 nc.sync.dma_start(out[P * n0 : P * (n0 + 2), cells].rearrange("(i p) c -> p i c", i=2), result[:])

from contextlib import ExitStack

import concourse.mybir as mybir
from concourse.masks import make_identity

K, M, H, N, S, T, T2 = 1024, 512, 1024, 512, 512, 2048, 1024
FLOPS = 2 * S * (K * M + M * H + 2 * K * H) + 2 * H * N * T2

F32 = mybir.dt.float32
BF16 = mybir.dt.bfloat16
I32 = mybir.dt.int32
U32 = mybir.dt.uint32
U16 = mybir.dt.uint16
U8 = mybir.dt.uint8
FP8X4 = mybir.dt.float8_e4m3fn_x4
FP4X4 = mybir.dt.float4_e2m1fn_x4
ACT = mybir.ActivationFunctionType
MULT = mybir.AluOpType.mult

P = 128
SLICES = H // P
PA_PAGES = 3
LAST_BYTES = 16 * T + 8 * S
WO_BYTES = LAST_BYTES + 4 * S
WEIGHTED_ON_GPSIMD = (3, 4)
WR_PIECES = ((0, 2), (2, 8))


def tile_list_ice_chart_features_kernel(
    tc, tab_words, tab_scales, tab2_words, tab2_scales, offs, offs2, offs3, offs4, w1, gain, w2,
    w3_words, w3_scales, wr_words, wr_scales, wg1, wg2, clim, wo, out,
):
    nc = tc.nc
    with ExitStack() as ctx:
        keep = ctx.enter_context(tc.tile_pool(name="keep", bufs=1))
        ring = ctx.enter_context(tc.tile_pool(name="ring", bufs=1))
        reused = ctx.enter_context(tc.tile_pool(name="reused", bufs=1))
        psum = ctx.enter_context(tc.psum_pool(name="psum", bufs=1))

        def kept(name, shape, dtype):
            return keep.tile(shape, dtype, name=name, align_bytes=64)

        def staged(name, shape, dtype):
            return ring.tile(shape, dtype, name=name, tag="stage", bufs=4, align_bytes=64)

        def bank(name):
            return psum.tile([P, 512], F32, name=name, tag="mm", bufs=4)

        lists = {}

        def load_list(name, src):
            lists[name] = kept(name, [P, S // 16], U16)
            nc.sync.dma_start(lists[name][:], src)

        def load_packed_scales(tile, src):
            for q in range(4):
                nc.sync.dma_start(tile[32 * q : 32 * q + 8, :].bitcast(I32), src[:, 4 * q : 4 * q + 4, :].bitcast(I32))

        def load_scales(tile, src):
            for q in range(4):
                nc.sync.dma_start(
                    tile[32 * q : 32 * q + 4, :, :].bitcast(I32),
                    src[:, 4 * q : 4 * q + 4, :].rearrange("a r c -> r a c").bitcast(I32),
                )

        def load_table_pass(window, words, a):
            nc.sync.dma_start(window[:].bitcast(I32), words[a].rearrange("p t i -> p (t i)").bitcast(I32))
            return window

        def load_rows(name, rows):
            raw = staged(name, [P, 4, 512], F32)
            nc.sync.dma_start(raw[:], rows.rearrange("(p j) c -> p j c", j=4))
            return raw

        wr = {}

        def load_wr(first, last):
            piece = kept("wr%d" % first, [P, 2, P * (last - first)], U32)
            src = wr_words.rearrange("a p c i -> p a (c i)")[:, :, 4 * P * first : 4 * P * last]
            nc.sync.dma_start(piece[:].bitcast(I32), src.bitcast(I32))
            for s in range(first, last):
                wr[s] = [piece[:, a, P * (s - first) : P * (s - first + 1)] for a in range(2)]

        def window(name, slot):
            return reused.tile([P, T], U32, name=name, offset=4 * T * slot)

        def late_pages(name, slot):
            pages = [
                reused.tile([P, T2], F32, name="%s%d" % (name, i), offset=4 * T * slot + 4 * T2 * i) for i in range(2)
            ]
            for page in pages:
                nc.gpsimd.memset(page[:].bitcast(I32), 0)
            return pages

        def load_clim(s):
            rows = ring.tile([P, T2], F32, name="clim%d" % s, tag="clim", bufs=3)
            nc.sync.dma_start(rows[:], clim[P * s : P * (s + 1), :])
            return rows

        tab2_sc = kept("tab2_sc", [P, T], U8)
        wr_sc = kept("wr_sc", [P, H], U8)
        tab_sc = kept("tab_sc", [P, T], U8)
        v_sc1 = kept("v_sc1", [P, S], U8)
        w3_sc = kept("w3_sc", [P, 2, H], U8)
        nc.vector.memset(tab2_sc[:].bitcast(I32), 0)
        nc.vector.memset(wr_sc[:].bitcast(I32), 0)
        pb_pages = [kept("pb%d" % i, [P, T2], F32) for i in range(2)]
        for page in pb_pages:
            nc.vector.memset(page[:].bitcast(I32), 0)
        nc.gpsimd.memset(tab_sc[:].bitcast(I32), 0)
        nc.gpsimd.memset(w3_sc[:].bitcast(I32), 0)
        nc.gpsimd.memset(v_sc1[:].bitcast(I32), 0)
        pa_pages = [kept("pa_early", [P, T2], F32)]
        nc.gpsimd.memset(pa_pages[0][:].bitcast(I32), 0)
        ident = kept("ident", [P, P], F32)
        make_identity(nc, ident[:])

        load_list("offs2", offs2)
        tab2_win = [load_table_pass(window("tab2_0", 0), tab2_words, 0)]
        load_packed_scales(tab2_sc, tab2_scales)
        tab2_win.append(load_table_pass(window("tab2_1", 1), tab2_words, 1))
        load_wr(*WR_PIECES[0])
        load_packed_scales(wr_sc, wr_scales)
        load_list("offs4", offs4)
        wg2_sb = kept("wg2", [P, S], F32)
        nc.sync.dma_start(wg2_sb[:], wg2)
        w1_raw = [load_rows("w1_%d" % a, w1[512 * a : 512 * (a + 1), :]) for a in range(2)]
        load_list("offs", offs)
        tab_win = [load_table_pass(window("tab_0", 2), tab_words, 0)]
        load_packed_scales(tab_sc, tab_scales)
        w2_raw = [load_rows("w2_0", w2[:, 0:512])]
        tab_win.append(load_table_pass(window("tab_1", 3), tab_words, 1))
        load_wr(*WR_PIECES[1])
        gain_sb = kept("gain", [P, 4], F32)
        nc.sync.dma_start(gain_sb[:], gain.rearrange("(p t) -> p t", t=4))
        w2_raw.append(load_rows("w2_1", w2[:, 512:1024]))
        load_scales(w3_sc, w3_scales)
        w3 = kept("w3", [P, 2, 2 * H], U8)
        nc.sync.dma_start(w3[:].bitcast(I32), w3_words.rearrange("a p c -> p a c").bitcast(I32))
        load_list("offs3", offs3)
        wg1_sb = kept("wg1", [P, S], F32)
        nc.sync.dma_start(wg1_sb[:], wg1)
        wo_raw = [load_rows("wo_%d" % g, wo[512 * g : 512 * (g + 1), :]) for g in range(2)]
        clim_sb = [load_clim(s) for s in range(SLICES)]

        def gather(name, window, list_name, dtype):
            picked = kept(name, [P, S], dtype)
            nc.vector.tensor_copy(picked[:], window.indirect(lists[list_name][:]))
            return picked

        def grouped_tile(name):
            return ring.tile([P, 2048], BF16, name=name, tag="grouped", bufs=3, align_bytes=64)

        def interleave(grouped, rows):
            nc.scalar.copy(
                grouped.rearrange("p (c i j) -> p c j i", i=4, j=4),
                rows.rearrange("p j (c i) -> p c j i", i=4),
            )

        def quantise(name, grouped):
            codes = kept(name + "_codes", [P, 512], U32)
            scales = kept(name + "_scales", [P, 512], U8)
            nc.vector.quantize_mx(codes[:].bitcast(FP8X4), scales[:], grouped[:])
            return codes, scales

        def place_pb(s, h2, parts=1):
            width = S // parts
            for i in range(parts):
                picks = slice(width * i, width * (i + 1))
                acc = bank("h2_acc%d%d" % (s, i))
                for a in range(2):
                    nc.tensor.matmul_mx(
                        acc[:, :width], wr[s][a].bitcast(FP8X4), wr_sc[4 * a :, P * s : P * (s + 1)],
                        v2[a][:, picks].bitcast(FP8X4), v2_sc[4 * a :, picks], start=(a == 0), stop=(a == 1),
                    )
                nc.scalar.activation(h2[:, picks], acc[:, :width], ACT.Tanh)
                offsets = lists["offs4"][:, width // 16 * i : width // 16 * (i + 1)]
                nc.vector.tensor_tensor(pb_pages[s][:].indirect(offsets), h2[:, picks], wg2_sb[:, picks], MULT)

        def h2_tile(s):
            return ring.tile([P, S], F32, name="h2_%d" % s, tag="h2", bufs=5)

        def place_pa(s):
            acc = bank("h1_acc%d" % s)
            for a in range(2):
                nc.tensor.matmul_mx(
                    acc[:], w3[:, a, 2 * P * s : 2 * P * (s + 1)].bitcast(FP4X4), w3_sc[:, a, P * s : P * (s + 1)],
                    v[a][:].bitcast(FP8X4), (v_sc, v_sc1)[a][:], start=(a == 0), stop=False,
                )
            codes, scales = w2_q[s // 4]
            cols = slice(P * (s % 4), P * (s % 4 + 1))
            nc.tensor.matmul_mx(
                acc[:], codes[:, cols].bitcast(FP8X4), scales[:, cols], act_q[0][:].bitcast(FP8X4), act_q[1][:],
                start=False, stop=True,
            )
            if s == 0:
                weighted = reused.tile([P, S], F32, name="weighted0", offset=WO_BYTES)
            elif s == SLICES - 1:
                weighted = reused.tile([P, S], F32, name="weighted%d" % s, offset=LAST_BYTES)
            else:
                weighted = ring.tile([P, S], F32, name="weighted%d" % s, tag="weighted", bufs=3)
            if s not in WEIGHTED_ON_GPSIMD:
                nc.vector.tensor_tensor(weighted[:], acc[:], wg1_sb[:], MULT)
            else:
                h1 = ring.tile([P, S], F32, name="h1_%d" % s, tag="h1", bufs=2)
                nc.scalar.copy(h1[:], acc[:])
                nc.gpsimd.tensor_tensor(weighted[:], h1[:], wg1_sb[:], MULT)
            nc.vector.tensor_copy(pa_pages[s % PA_PAGES][:].indirect(lists["offs3"][:]), weighted[:])

        z_t = [[kept("z_t%d%d" % (g, half), [P, 4, 2, 256], BF16) for half in range(2)] for g in range(2)]
        z_codes = [kept("z_codes%d" % g, [P, T2], U32) for g in range(2)]

        def turn_z_rows(s):
            pa, pb = pa_pages[s % PA_PAGES], pb_pages[s]
            if s + 1 < SLICES:
                whole = ring.tile([P, T2], F32, name="prod%d" % s, tag="prod", bufs=3)
                nc.gpsimd.tensor_tensor(whole[:], pa[:], pb[:], MULT)
            for half in range(2):
                cells = slice(512 * half, 512 * (half + 1))
                if s + 1 < SLICES:
                    prod = whole[:, cells]
                else:
                    prod = ring.tile([P, 512], F32, name="prod%d%d" % (s, half), tag="prod", bufs=3)
                    nc.vector.tensor_tensor(prod[:], pa[:, cells], pb[:, cells], MULT)
                turned = psum.tile([P, 4, P], F32, name="turned%d%d" % (s, half), tag="turned", bufs=2)
                for c in range(4):
                    first = 512 * half + P * c
                    nc.tensor.matmul(
                        turned[:, c, :], clim_sb[s][:, first : first + P], ident[:],
                        start=(c == 0), stop=False, is_transpose=True,
                    )
                for c in range(4):
                    nc.tensor.matmul(
                        turned[:, c, :], prod[:, P * c : P * (c + 1)], ident[:],
                        start=False, stop=(c == 3), is_transpose=True,
                    )
                place = slice(64 * (s % 4), 64 * (s % 4 + 1))
                nc.scalar.copy(
                    z_t[s // 4][half][:, :, :, place].rearrange("p c u (q e) -> p c u q e", e=2),
                    turned[:].rearrange("p c (q u e) -> p c u q e", u=2, e=2),
                )

        def turn_z_back(g, pair, grouped, copy_out):
            back = psum.tile([P, 2, 2, P], F32, name="back%d%d" % (g, pair), tag="back", bufs=2)
            words = z_t[g][pair // 2][:].bitcast(F32)
            for c in range(2):
                for u in range(2):
                    nc.tensor.transpose(back[:, c, u, :], words[:, 2 * (pair % 2) + c, u, :], ident[:])
            copy_out(
                grouped.bitcast(F32).rearrange("p (c r u) -> p c r u", c=2, u=2),
                back[:].rearrange("p c u r -> p c r u"),
            )

        v2 = [gather("v2_0", tab2_win[0][:], "offs2", U32)]
        v2_sc = gather("v2_sc", tab2_sc[:], "offs2", U8)
        v2.append(kept("v2_1", [P, S], U32))
        for i in range(2):
            nc.vector.tensor_copy(
                v2[1][:, 256 * i : 256 * (i + 1)], tab2_win[1][:].indirect(lists["offs2"][:, 16 * i : 16 * (i + 1)])
            )
        pb_pages.extend(late_pages("pb_a", 0) + late_pages("pb_b", 1))
        place_pb(0, h2_tile(0), parts=2)
        place_pb(1, h2_tile(1))

        w1_q = []
        for a in range(2):
            grouped = grouped_tile("w1_grouped%d" % a)
            nc.scalar.copy(
                grouped[:].rearrange("p (t q j) -> p q j t", t=4, j=4),
                w1_raw[a][:].rearrange("p j (q t) -> p q j t", t=4),
            )
            w1_q.append(quantise("w1_%d" % a, grouped))
        v = [gather("v_0", tab_win[0][:], "offs", U32)]
        v_sc = gather("v_sc", tab_sc[:], "offs", U8)
        for q in range(4):
            nc.sync.dma_start(v_sc1[32 * q : 32 * q + 4, :].bitcast(I32), v_sc[32 * q + 4 : 32 * q + 8, :].bitcast(I32))
        v.append(gather("v_1", tab_win[1][:], "offs", U32))
        pb_pages.extend(late_pages("pb_c", 2))
        pa_pages.extend(late_pages("pa", 3))
        w2_grouped = grouped_tile("w2_grouped0")
        interleave(w2_grouped[:], w2_raw[0][:])
        w2_q = [quantise("w2_0", w2_grouped)]
        for s in range(2, SLICES - 1):
            place_pb(s, h2_tile(s))
        act_rows = reused.tile([P, 4, S], BF16, name="act_rows", offset=16 * T)
        for t in range(4):
            acc = bank("act_acc%d" % t)
            cols = slice(P * t, P * (t + 1))
            for a in range(2):
                nc.tensor.matmul_mx(
                    acc[:], w1_q[a][0][:, cols].bitcast(FP8X4), w1_q[a][1][:, cols],
                    v[a][:].bitcast(FP8X4), v_sc[4 * a :, :], start=(a == 0), stop=(a == 1),
                )
            squashed = ring.tile([P, S], F32, name="squashed%d" % t, tag="squashed", bufs=2)
            nc.scalar.activation(squashed[:], acc[:], ACT.Tanh)
            nc.scalar.activation(act_rows[:, t, :], squashed[:], ACT.Copy, scale=gain_sb[:, t : t + 1])
        act_grouped = grouped_tile("act_grouped")
        interleave(act_grouped[:], act_rows[:])
        w2_grouped = grouped_tile("w2_grouped1")
        interleave(w2_grouped[:], w2_raw[1][:])
        w2_q.append(quantise("w2_1", w2_grouped))
        act_q = quantise("act", act_grouped)
        place_pb(SLICES - 1, reused.tile([P, S], F32, name="h2_last", offset=16 * T))

        wo_grouped = reused.tile([P, 2, 2048], BF16, name="wo_grouped", offset=WO_BYTES, align_bytes=64)
        z0_grouped = staged("z0_grouped", [P, 4, 1024], BF16)
        wo_codes = kept("wo_codes", [P, 2, N], U32)
        for g in range(2):
            interleave(wo_grouped[:, g, :], wo_raw[g][:])
        wo_scales = kept("wo_scales", [P, 2, N], U8)
        nc.vector.quantize_mx(
            wo_codes[:].rearrange("p g n -> p (g n)").bitcast(FP8X4),
            wo_scales[:].rearrange("p g n -> p (g n)"),
            wo_grouped[:].rearrange("p g c -> p (g c)"),
        )
        place_pa(0)
        place_pa(1)
        for s in range(SLICES):
            if s + 2 < SLICES:
                place_pa(s + 2)
            turn_z_rows(s)
            if s == 3:
                for pair in range(4):
                    turn_z_back(0, pair, z0_grouped[:, pair, :], nc.scalar.copy)
        z_scales = [
            reused.tile([P, T2], U8, name="z_scales0", offset=LAST_BYTES, align_bytes=64),
            kept("z_scales1", [P, T2], U8),
        ]
        nc.vector.quantize_mx(z_codes[0][:].bitcast(FP8X4), z_scales[0][:], z0_grouped[:].rearrange("p a c -> p (a c)"))

        for pair in range(4):
            cells = slice(256 * pair, 256 * (pair + 1))
            grouped = ring.tile([P, 1024], BF16, name="z_grouped%d" % pair, tag="z_grouped", bufs=3, align_bytes=64)
            turn_z_back(1, pair, grouped[:], nc.scalar.copy if pair == 1 else nc.vector.tensor_copy)
            nc.vector.quantize_mx(z_codes[1][:, cells].bitcast(FP8X4), z_scales[1][:, cells], grouped[:])
        for pair in range(4):
            cells = slice(256 * pair, 256 * (pair + 1))
            for n0 in range(0, N // P, 2):
                acc = bank("y_acc%d%d" % (pair, n0))
                for g in range(2):
                    for i in range(2):
                        cols = slice(P * (n0 + i), P * (n0 + i + 1))
                        nc.tensor.matmul_mx(
                            acc[:, 256 * i : 256 * (i + 1)], wo_codes[:, g, cols].bitcast(FP8X4), wo_scales[:, g, cols],
                            z_codes[g][:, cells].bitcast(FP8X4), z_scales[g][:, cells], start=(g + i == 0), stop=(g + i == 2),
                        )
                result = reused.tile([P, 2, 256], F32, name="result%d%d" % (pair, n0), offset=2048 * (2 * pair + n0 // 2))
                nc.scalar.activation(result[:], acc[:].rearrange("p (i c) -> p i c", i=2), ACT.Abs)
                nc.sync.dma_start(out[P * n0 : P * (n0 + 2), cells].rearrange("(i p) c -> p i c", i=2), result[:])
